import numpy as np
import ml_dtypes


def mxq(x, axis, fmt="e4m3"):
    dtype, down = {"e4m3": (ml_dtypes.float8_e4m3fn, 7), "e5m2": (ml_dtypes.float8_e5m2, 14)}[fmt]
    v = np.moveaxis(np.asarray(x, np.float32).astype(ml_dtypes.bfloat16).astype(np.float64), axis, -1)
    blocks = v.reshape(v.shape[:-1] + (-1, 32))
    amax = np.abs(blocks).max(-1, keepdims=True)
    byte = np.maximum(np.where(amax > 0, np.frexp(amax)[1] - 1 + 127, 0) - down, 1)
    scale = np.exp2(byte - 127.0)
    codes = (blocks / scale).astype(np.float32).astype(dtype).astype(np.float64)
    return np.moveaxis((codes * scale).reshape(v.shape), -1, axis)


WIDE = False


def mx_kscale(k):
    if not WIDE:
        return np.ones(k)
    levels = np.array([10, -10, 5, -5, 0])
    if k % 512:
        return np.exp2(np.random.permutation(np.resize(levels, k // 32))).repeat(32)
    a = np.empty((k // 512, 16))
    for p in range(k // 512):
        a[p, :8] = np.random.permutation(np.resize(levels, 8))
        for g in range(8):
            far = levels[np.abs(levels - a[p, g]) >= 10]
            a[p, g + 8] = far[np.random.randint(len(far))]
    return np.exp2(a.ravel()).repeat(32)


def f64(x):
    return np.asarray(x).astype(np.float64)


def striped(idx):
    return np.tile(idx.reshape(-1, 16).T, (8, 1)).astype(np.uint16)


def unstriped(offs):
    return offs[:16].T.reshape(-1).astype(np.int64)


def pack_weight(w):
    k, n = w.shape
    w = f64(np.asarray(w, np.float32).astype(ml_dtypes.bfloat16)).reshape(k // 32, 32, n)
    amax = np.abs(w).max(1)
    byte = np.clip(np.where(amax > 0, np.frexp(amax)[1] - 1 + 127 - 7, 1), 1, 254)
    scaled = (w * np.exp2(127.0 - byte)[:, None, :]).reshape(k, n).astype(np.float32)
    words = np.ascontiguousarray(scaled.reshape(k // 512, 128, 4, n).transpose(0, 1, 3, 2)).astype(ml_dtypes.float8_e4m3fn).view(np.uint8)
    return words, np.ascontiguousarray(byte.astype(np.uint8).reshape(k // 512, 16, n))


def unpack_weight(words, scales):
    g, p, n, _ = words.shape
    vals = np.ascontiguousarray(words).view(ml_dtypes.float8_e4m3fn).astype(np.float64) * np.repeat(np.exp2(scales.astype(np.float64) - 127.0), 8, axis=1)[..., None]
    return vals.transpose(0, 1, 3, 2).reshape(g * 512, n)


K, T, S, D, N, V = 512, 2048, 512, 4, 256, 128
P = 2 ** 7


def setup_inputs():
    n = np.random.standard_normal
    s = mx_kscale(K)[:, None]
    packed_xT = pack_weight(n((K, T)) * s)
    return {
        "x_words": packed_xT[0],
        "x_scales": packed_xT[1],
        "w1": (n((K, N)) / np.sqrt(K) / s).astype(np.float32),
        "w2": (n((K, N)) / np.sqrt(K) / s).astype(np.float32),
        "trt": (np.tile((np.random.uniform(size=S) < 0.5) * 1.0, (P, 1))).astype(np.float32),
        "cap": (np.tile(np.random.uniform(1.5, 4.0, V), (P, 1))).astype(np.float32),
        "obs": (n((N, V))).astype(np.float32),
        "eff": (n((N, 1))).astype(np.float32),
        "offs": striped(np.random.permutation(T)[:S]),
    }


def reference(x_words, x_scales, w1, w2, trt, cap, obs, eff, offs):
    xq = unpack_weight(x_words, x_scales)[:, unstriped(offs)]
    yn = mxq(f64(w1), 0, "e4m3").T @ xq
    yd = mxq(f64(w2), 0, "e4m3").T @ xq
    lr = f64(trt)[:1] * yn - (np.log(np.exp(yn) + 1.0)) - (f64(trt)[:1] * yd - (np.log(np.exp(yd) + 1.0)))
    lw = lr.reshape(len(lr), -1, D).sum(axis=2)
    wt = np.minimum(np.exp(lw), f64(cap)[:1])
    return wt * ((f64(obs) - (f64(eff) * (f64(trt)[:1].reshape(len(f64(trt)[:1]), -1, D).mean(axis=2)))) ** 2)

@@ -1,0 +1,213 @@
+import math
+from contextlib import ExitStack
+
+import concourse.mybir as mybir
+from concourse.masks import make_identity
+
+F32 = mybir.dt.float32
+BF16 = mybir.dt.bfloat16
+I32 = mybir.dt.int32
+U32 = mybir.dt.uint32
+U16 = mybir.dt.uint16
+U8 = mybir.dt.uint8
+FP8X4 = mybir.dt.float8_e4m3fn_x4
+ALU = mybir.AluOpType
+ACT = mybir.ActivationFunctionType
+
+P = 128
+PACK = 4
+K, T, S, D, N, V = 512, 2048, 512, 4, 256, 128
+BLOCKS = N // P
+CLIP = 16.0
+BIG = 3.0e38
+SPLIT = 96
+
+FLOPS = 2 * 2 * K * N * S
+
+
+def tile_picked_ymsmw_loss_p_kernel(
+    tc, x_words, x_scales, w1, w2, trt, cap, obs, eff, offs, out
+):
+    nc = tc.nc
+    with ExitStack() as ctx:
+        sb = ctx.enter_context(tc.tile_pool(name="sb", bufs=1))
+        ps = ctx.enter_context(tc.psum_pool(name="ps", bufs=1))
+
+        def tile(name, shape, dtype):
+            return sb.tile(shape, dtype, name=name, align_bytes=64)
+
+        offsets = tile("offsets", [P, S // 16], U16)
+        nc.sync.dma_start(offsets[:], offs)
+
+        table_scales = tile("table_scales", [P, T], U8)
+        nc.vector.memset(table_scales[:].bitcast(I32), 0)
+        treated = tile("treated", [P, D], F32)
+        nc.sync.dma_start(treated[:], trt[0].rearrange("(v d) -> v d", d=D))
+        effect = tile("effect", [P, BLOCKS, 1], F32)
+        with nc.allow_non_contiguous_dma(reason="one value a partition and block"):
+            nc.gpsimd.dma_start(effect[:], eff.rearrange("(b p) o -> p b o", p=P))
+        raw_d = tile("raw_d", [P, PACK, N], F32)
+        nc.sync.dma_start(raw_d[:], w2.rearrange("(p j) m -> p j m", j=PACK))
+        for q in range(4):
+            nc.sync.dma_start(
+                table_scales[32 * q : 32 * q + 4, :].bitcast(I32),
+                x_scales[0, 4 * q : 4 * q + 4, :].bitcast(I32),
+            )
+        table_words = tile("table_words", [P, T], I32)
+        nc.sync.dma_start(table_words[:], x_words[0].rearrange("p c r -> p (c r)").bitcast(I32))
+        raw_n = tile("raw_n", [P, PACK, N], F32)
+        nc.sync.dma_start(raw_n[:], w1.rearrange("(p j) m -> p j m", j=PACK))
+        outcome = tile("outcome", [P, BLOCKS, V], F32)
+        nc.sync.dma_start(outcome[:], obs.rearrange("(b p) v -> p b v", p=P))
+        cap_col = tile("cap_col", [P, 1], F32)
+        with nc.allow_non_contiguous_dma(reason="one value a partition"):
+            nc.sync.dma_start(cap_col[:], cap[0].rearrange("(v o) -> v o", o=1))
+
+        ident = tile("ident", [P, P], F32)
+        make_identity(nc, ident[:])
+
+        sign = tile("sign", [P, D], F32)
+        neg_sign = tile("neg_sign", [P, D], F32)
+        nc.scalar.activation(neg_sign[:], treated[:], ACT.Copy, bias=1.0, scale=-2.0)
+        nc.scalar.activation(sign[:], treated[:], ACT.Copy, bias=-1.0, scale=2.0)
+        neg_clip = tile("neg_clip", [P, 1], F32)
+        nc.gpsimd.memset(neg_clip[:], -CLIP)
+
+        picked_scales = tile("picked_scales", [P, S], U8)
+        nc.vector.tensor_copy(picked_scales[:], table_scales[:].indirect(offsets[:]))
+        visit_scales = tile("visit_scales", [P, D, V], U8)
+        nc.vector.tensor_copy(visit_scales[:], picked_scales[:].rearrange("p (v d) -> p d v", d=D))
+
+        share = tile("share", [P, D], F32)
+        neg_mean = tile("neg_mean", [P, 1], F32)
+        nc.scalar.activation(share[:], treated[:], ACT.Copy, scale=-1.0 / D, accum_out=neg_mean[:])
+        spread = ps.tile([P, V], F32, name="yn0")
+        nc.tensor.transpose(spread[:], neg_mean[:].to_broadcast([P, P]), ident[:])
+        shift = tile("shift", [P, BLOCKS, V], F32)
+        for b in range(BLOCKS):
+            nc.scalar.activation(shift[:, b, :], spread[:], ACT.Copy, scale=effect[:, b, :])
+
+        def interleave(copy, grouped, raw, lo, hi):
+            copy(
+                grouped[:, lo:hi, :].rearrange("p (c i) j -> p c j i", i=4),
+                raw[:, :, lo:hi].rearrange("p j (c i) -> p c j i", i=4),
+            )
+
+        def quantize(name, grouped):
+            codes = tile(name + "_codes", [P, N], U32)
+            scales = tile(name + "_scales", [P, N], U8)
+            nc.vector.quantize_mx(
+                out=codes[:].bitcast(FP8X4), scales=scales[:], in_=grouped[:].rearrange("p m j -> p (m j)")
+            )
+            return codes, scales
+
+        def products(name, codes, scales):
+            banks = [ps.tile([P, 2, N], F32, name="%s%d" % (name, h)) for h in range(2)]
+            for d in range(D):
+                nc.tensor.matmul_mx(
+                    out=banks[d // 2][:, d % 2, :],
+                    lhsT=visit_words[:, d, :].bitcast(FP8X4),
+                    lhsT_scale=visit_scales[:, d, :],
+                    rhs=codes[:].bitcast(FP8X4),
+                    rhs_scale=scales[:],
+                    start=True,
+                    stop=True,
+                )
+            return banks
+
+        grouped_d = tile("grouped_d", [P, N, PACK], BF16)
+        interleave(nc.scalar.copy, grouped_d, raw_d, 0, N)
+        codes_d, scales_d = quantize("wd", grouped_d)
+
+        visit_words = tile("visit_words", [P, D, V], U32)
+        nc.vector.tensor_copy(
+            visit_words[:].rearrange("p d v -> p v d"), table_words[:].bitcast(U32).indirect(offsets[:])
+        )
+
+        yd = products("yd", codes_d, scales_d)
+
+        grouped_n = tile("grouped_n", [P, N, PACK], BF16)
+        interleave(nc.scalar.copy, grouped_n, raw_n, 0, SPLIT)
+        interleave(nc.vector.tensor_copy, grouped_n, raw_n, SPLIT, N)
+        codes_n, scales_n = quantize("wn", grouped_n)
+        yn = products("yn", codes_n, scales_n)
+
+        log_part = [ps.tile([P, V], F32, name="log_part%d" % b) for b in range(BLOCKS)]
+
+        def add_turned(src, first, last):
+            for b in range(BLOCKS):
+                nc.tensor.matmul(
+                    log_part[b][:], src[:, b * P : (b + 1) * P], ident[:], start=first, stop=last, is_transpose=True
+                )
+
+        odds = [tile("odds%d" % d, [P, N], F32) for d in range(D)]
+        inv_chance = [tile("inv_chance%d" % d, [P, N], F32) for d in range(D)]
+        excess = [tile("excess%d" % d, [P, N], F32) for d in range(D)]
+        deficit = [tile("deficit%d" % d, [P, N], F32) for d in range(D)]
+        for d in range(D):
+            nc.scalar.activation(odds[d][:], yd[d // 2][:, d % 2, :], ACT.Exp, scale=neg_sign[:, d : d + 1])
+            nc.vector.tensor_scalar(inv_chance[d][:], odds[d][:], math.exp(CLIP), 1.0, ALU.min, ALU.add)
+        pair = [tile("pair%d" % h, [P, N], F32) for h in range(2)]
+        for h in range(2):
+            nc.vector.tensor_tensor(pair[h][:], inv_chance[2 * h][:], inv_chance[2 * h + 1][:], ALU.mult)
+        for d in range(D):
+            nc.scalar.activation(
+                excess[d][:], yd[d // 2][:, d % 2, :], ACT.Relu, scale=neg_sign[:, d : d + 1], bias=neg_clip[:]
+            )
+            add_turned(excess[d], d == 0, False)
+        for d in range(D):
+            nc.vector.tensor_scalar(deficit[d][:], yn[d // 2][:, d % 2, :], sign[:, d : d + 1], 0.0, ALU.mult, ALU.min)
+            add_turned(deficit[d], False, d == D - 1)
+
+        resid = ps.tile([P, BLOCKS, P], F32, name="resid")
+        for b in range(BLOCKS):
+            nc.tensor.matmul(resid[:, b, :], outcome[:, b, :], ident[:], start=True, stop=False, is_transpose=True)
+            nc.tensor.matmul(resid[:, b, :], shift[:, b, :], ident[:], start=False, stop=True, is_transpose=True)
+        square = tile("square", [P, N], F32)
+        nc.scalar.activation(square[:], resid[:].rearrange("p b m -> p (b m)"), ACT.Square)
+
+        half_abs = [tile("half_abs%d" % h, [P, 2, N], F32) for h in range(2)]
+        tanh = [tile("tanh%d" % d, [P, N], F32) for d in range(D)]
+        step = [tile("step%d" % d, [P, N], F32) for d in range(D)]
+        scaled = tile("scaled", [P, N], F32)
+        joined = tile("joined", [P, N], F32)
+        nc.vector.scalar_tensor_tensor(scaled[:], pair[1][:], 0.5**D, square[:], ALU.mult, ALU.mult)
+        for h in range(2):
+            nc.scalar.activation(half_abs[h][:], yn[h][:], ACT.Abs, scale=0.5)
+            if h == 0:
+                for d in range(2):
+                    nc.scalar.activation(tanh[d][:], half_abs[0][:, d, :], ACT.Tanh)
+        nc.vector.scalar_tensor_tensor(step[0][:], tanh[0][:], 1.0, pair[0][:], ALU.add, ALU.mult)
+        nc.vector.scalar_tensor_tensor(step[1][:], tanh[1][:], 1.0, scaled[:], ALU.add, ALU.mult)
+        nc.scalar.activation(tanh[2][:], half_abs[1][:, 0, :], ACT.Tanh)
+        halves = [slice(b * P, (b + 1) * P) for b in range(BLOCKS)]
+        for cols in halves:
+            nc.scalar.activation(tanh[3][:, cols], half_abs[1][:, 1, cols], ACT.Tanh)
+        for cols in halves:
+            nc.vector.tensor_tensor(joined[:, cols], step[0][:, cols], step[1][:, cols], ALU.mult)
+        for cols in halves:
+            nc.vector.scalar_tensor_tensor(step[2][:, cols], tanh[2][:, cols], 1.0, joined[:, cols], ALU.add, ALU.mult)
+        for cols in halves:
+            nc.vector.scalar_tensor_tensor(step[3][:, cols], tanh[3][:, cols], 1.0, step[2][:, cols], ALU.add, ALU.mult)
+        running = step[3]
+
+        capped = tile("capped", [P, N], F32)
+        nc.scalar.activation(capped[:], square[:], ACT.Copy, scale=cap_col[:])
+        cap_sq = ps.tile([P, BLOCKS, V], F32, name="cap_sq")
+        for b in range(BLOCKS):
+            nc.tensor.transpose(cap_sq[:, b, :], capped[:, b * P : (b + 1) * P], ident[:])
+
+        growth = tile("growth", [P, BLOCKS, V], F32)
+        for b in range(BLOCKS):
+            nc.scalar.activation(growth[:, b, :], log_part[b][:], ACT.Exp)
+
+        turned = [ps.tile([P, V], F32, name=nm) for nm in ("yd0", "yd1")]
+        weighted = tile("weighted", [P, BLOCKS, V], F32)
+        result = tile("result", [P, BLOCKS, V], F32)
+        for b in range(BLOCKS):
+            nc.tensor.transpose(turned[b][:], running[:, b * P : (b + 1) * P], ident[:])
+        for b in range(BLOCKS):
+            nc.vector.scalar_tensor_tensor(weighted[:, b, :], growth[:, b, :], BIG, turned[b][:], ALU.min, ALU.mult)
+        for b in range(BLOCKS):
+            nc.vector.tensor_tensor(result[:, b, :], weighted[:, b, :], cap_sq[:, b, :], ALU.min)
+        nc.sync.dma_start(out.rearrange("(b p) v -> p b v", p=P), result[:])

@@ -20,7 +20,6 @@ K, T, S, D, N, V = 512, 2048, 512, 4, 256, 128
 BLOCKS = N // P
 CLIP = 16.0
 BIG = 3.0e38
-SPLIT = 96
 
 FLOPS = 2 * 2 * K * N * S
 
@@ -31,6 +30,7 @@ def tile_picked_ymsmw_loss_p_kernel(
     nc = tc.nc
     with ExitStack() as ctx:
         sb = ctx.enter_context(tc.tile_pool(name="sb", bufs=1))
+        reuse = ctx.enter_context(tc.tile_pool(name="reuse", bufs=1))
         ps = ctx.enter_context(tc.psum_pool(name="ps", bufs=1))
 
         def tile(name, shape, dtype):
@@ -40,28 +40,27 @@ def tile_picked_ymsmw_loss_p_kernel(
         nc.sync.dma_start(offsets[:], offs)
 
         table_scales = tile("table_scales", [P, T], U8)
-        nc.vector.memset(table_scales[:].bitcast(I32), 0)
+        for q in range(4):
+            nc.sync.dma_start(
+                table_scales[32 * q : 32 * q + 32, :].bitcast(I32),
+                x_scales[0, 4 * q : 4 * q + 4, :].bitcast(I32).partition_broadcast(8),
+            )
         treated = tile("treated", [P, D], F32)
         nc.sync.dma_start(treated[:], trt[0].rearrange("(v d) -> v d", d=D))
         effect = tile("effect", [P, BLOCKS, 1], F32)
         with nc.allow_non_contiguous_dma(reason="one value a partition and block"):
-            nc.gpsimd.dma_start(effect[:], eff.rearrange("(b p) o -> p b o", p=P))
+            nc.sync.dma_start(effect[:], eff.rearrange("(b p) o -> p b o", p=P))
+        table_words = reuse.tile([P, T], I32, name="table_words", align_bytes=64, offset=0)
+        nc.sync.dma_start(table_words[:], x_words[0].rearrange("p c r -> p (c r)").bitcast(I32))
         raw_d = tile("raw_d", [P, PACK, N], F32)
         nc.sync.dma_start(raw_d[:], w2.rearrange("(p j) m -> p j m", j=PACK))
-        for q in range(4):
-            nc.sync.dma_start(
-                table_scales[32 * q : 32 * q + 4, :].bitcast(I32),
-                x_scales[0, 4 * q : 4 * q + 4, :].bitcast(I32),
-            )
-        table_words = tile("table_words", [P, T], I32)
-        nc.sync.dma_start(table_words[:], x_words[0].rearrange("p c r -> p (c r)").bitcast(I32))
-        raw_n = tile("raw_n", [P, PACK, N], F32)
-        nc.sync.dma_start(raw_n[:], w1.rearrange("(p j) m -> p j m", j=PACK))
         outcome = tile("outcome", [P, BLOCKS, V], F32)
         nc.sync.dma_start(outcome[:], obs.rearrange("(b p) v -> p b v", p=P))
         cap_col = tile("cap_col", [P, 1], F32)
         with nc.allow_non_contiguous_dma(reason="one value a partition"):
             nc.sync.dma_start(cap_col[:], cap[0].rearrange("(v o) -> v o", o=1))
+        raw_n = tile("raw_n", [P, PACK, N], F32)
+        nc.sync.dma_start(raw_n[:], w1.rearrange("(p j) m -> p j m", j=PACK))
 
         ident = tile("ident", [P, P], F32)
         make_identity(nc, ident[:])
@@ -87,50 +86,68 @@ def tile_picked_ymsmw_loss_p_kernel(
         for b in range(BLOCKS):
             nc.scalar.activation(shift[:, b, :], spread[:], ACT.Copy, scale=effect[:, b, :])
 
-        def interleave(copy, grouped, raw, lo, hi):
-            copy(
-                grouped[:, lo:hi, :].rearrange("p (c i) j -> p c j i", i=4),
-                raw[:, :, lo:hi].rearrange("p j (c i) -> p c j i", i=4),
-            )
-
-        def quantize(name, grouped):
-            codes = tile(name + "_codes", [P, N], U32)
-            scales = tile(name + "_scales", [P, N], U8)
-            nc.vector.quantize_mx(
-                out=codes[:].bitcast(FP8X4), scales=scales[:], in_=grouped[:].rearrange("p m j -> p (m j)")
-            )
-            return codes, scales
-
-        def products(name, codes, scales):
-            banks = [ps.tile([P, 2, N], F32, name="%s%d" % (name, h)) for h in range(2)]
-            for d in range(D):
-                nc.tensor.matmul_mx(
-                    out=banks[d // 2][:, d % 2, :],
-                    lhsT=visit_words[:, d, :].bitcast(FP8X4),
-                    lhsT_scale=visit_scales[:, d, :],
-                    rhs=codes[:].bitcast(FP8X4),
-                    rhs_scale=scales[:],
-                    start=True,
-                    stop=True,
-                )
-            return banks
-
-        grouped_d = tile("grouped_d", [P, N, PACK], BF16)
-        interleave(nc.scalar.copy, grouped_d, raw_d, 0, N)
-        codes_d, scales_d = quantize("wd", grouped_d)
+        resid = ps.tile([P, BLOCKS, P], F32, name="yn1")
+        for b in range(BLOCKS):
+            nc.tensor.matmul(resid[:, b, :], outcome[:, b, :], ident[:], start=True, stop=False, is_transpose=True)
+            nc.tensor.matmul(resid[:, b, :], shift[:, b, :], ident[:], start=False, stop=True, is_transpose=True)
 
         visit_words = tile("visit_words", [P, D, V], U32)
         nc.vector.tensor_copy(
             visit_words[:].rearrange("p d v -> p v d"), table_words[:].bitcast(U32).indirect(offsets[:])
         )
 
-        yd = products("yd", codes_d, scales_d)
+        halves = [slice(b * P, (b + 1) * P) for b in range(BLOCKS)]
 
-        grouped_n = tile("grouped_n", [P, N, PACK], BF16)
-        interleave(nc.scalar.copy, grouped_n, raw_n, 0, SPLIT)
-        interleave(nc.vector.tensor_copy, grouped_n, raw_n, SPLIT, N)
-        codes_n, scales_n = quantize("wn", grouped_n)
-        yn = products("yn", codes_n, scales_n)
+        def interleave(copy, grouped, raw, cols):
+            copy(
+                grouped[:].rearrange("p (c i) j -> p c j i", i=4),
+                raw[:, :, cols].rearrange("p j (c i) -> p c j i", i=4),
+            )
+
+        def quantize(codes, scales, grouped, cols):
+            nc.vector.quantize_mx(
+                out=codes[:, cols].bitcast(FP8X4), scales=scales[:, cols], in_=grouped[:].rearrange("p m j -> p (m j)")
+            )
+
+        def product(bank, d, codes, scales):
+            nc.tensor.matmul_mx(
+                out=bank,
+                lhsT=visit_words[:, d, :].bitcast(FP8X4),
+                lhsT_scale=visit_scales[:, d, :],
+                rhs=codes[:].bitcast(FP8X4),
+                rhs_scale=scales[:],
+                start=True,
+                stop=True,
+            )
+
+        stage_s = reuse.tile([P, P, PACK], BF16, name="stage_sd", align_bytes=64, offset=8192)
+        stage_v = reuse.tile([P, P, PACK], BF16, name="stage_vd", align_bytes=64, offset=7168)
+        codes_d = reuse.tile([P, N], U32, name="codes_d", align_bytes=64, offset=2048)
+        scales_d = tile("scales_d", [P, N], U8)
+        interleave(nc.scalar.copy, stage_s, raw_d, halves[0])
+        interleave(nc.vector.tensor_copy, stage_v, raw_d, halves[1])
+        quantize(codes_d, scales_d, stage_s, halves[0])
+        quantize(codes_d, scales_d, stage_v, halves[1])
+        yd = [ps.tile([P, N], F32, name="yd%d" % d) for d in range(D)]
+        for d in range(D):
+            product(yd[d][:], d, codes_d, scales_d)
+
+        square = tile("raw_d", [P, N], F32)
+        nc.scalar.activation(square[:], resid[:].rearrange("p b m -> p (b m)"), ACT.Square)
+        capped = tile("capped", [P, N], F32)
+        nc.scalar.activation(capped[:], square[:], ACT.Copy, scale=cap_col[:])
+
+        stage_s = tile("stage_n", [P, P, PACK], BF16)
+        stage_v = reuse.tile([P, P, PACK], BF16, name="stage_vn", align_bytes=64, offset=7680)
+        codes_n = reuse.tile([P, N], U32, name="codes_n", align_bytes=64, offset=8704)
+        scales_n = reuse.tile([P, N], U8, name="scales_n", align_bytes=64, offset=7168)
+        interleave(nc.scalar.copy, stage_s, raw_n, halves[0])
+        interleave(nc.vector.tensor_copy, stage_v, raw_n, halves[1])
+        quantize(codes_n, scales_n, stage_s, halves[0])
+        quantize(codes_n, scales_n, stage_v, halves[1])
+        yn = [ps.tile([P, 2, N], F32, name="yn%d" % h) for h in range(2)]
+        for d in range(D):
+            product(yn[d // 2][:, d % 2, :], d, codes_n, scales_n)
 
         log_part = [ps.tile([P, V], F32, name="log_part%d" % b) for b in range(BLOCKS)]
 
@@ -145,26 +162,19 @@ def tile_picked_ymsmw_loss_p_kernel(
         excess = [tile("excess%d" % d, [P, N], F32) for d in range(D)]
         deficit = [tile("deficit%d" % d, [P, N], F32) for d in range(D)]
         for d in range(D):
-            nc.scalar.activation(odds[d][:], yd[d // 2][:, d % 2, :], ACT.Exp, scale=neg_sign[:, d : d + 1])
+            nc.scalar.activation(odds[d][:], yd[d][:], ACT.Exp, scale=neg_sign[:, d : d + 1])
             nc.vector.tensor_scalar(inv_chance[d][:], odds[d][:], math.exp(CLIP), 1.0, ALU.min, ALU.add)
         pair = [tile("pair%d" % h, [P, N], F32) for h in range(2)]
         for h in range(2):
             nc.vector.tensor_tensor(pair[h][:], inv_chance[2 * h][:], inv_chance[2 * h + 1][:], ALU.mult)
         for d in range(D):
             nc.scalar.activation(
-                excess[d][:], yd[d // 2][:, d % 2, :], ACT.Relu, scale=neg_sign[:, d : d + 1], bias=neg_clip[:]
+                excess[d][:], yd[d][:], ACT.Relu, scale=neg_sign[:, d : d + 1], bias=neg_clip[:]
             )
             add_turned(excess[d], d == 0, False)
         for d in range(D):
             nc.vector.tensor_scalar(deficit[d][:], yn[d // 2][:, d % 2, :], sign[:, d : d + 1], 0.0, ALU.mult, ALU.min)
             add_turned(deficit[d], False, d == D - 1)
-
-        resid = ps.tile([P, BLOCKS, P], F32, name="resid")
-        for b in range(BLOCKS):
-            nc.tensor.matmul(resid[:, b, :], outcome[:, b, :], ident[:], start=True, stop=False, is_transpose=True)
-            nc.tensor.matmul(resid[:, b, :], shift[:, b, :], ident[:], start=False, stop=True, is_transpose=True)
-        square = tile("square", [P, N], F32)
-        nc.scalar.activation(square[:], resid[:].rearrange("p b m -> p (b m)"), ACT.Square)
 
         half_abs = [tile("half_abs%d" % h, [P, 2, N], F32) for h in range(2)]
         tanh = [tile("tanh%d" % d, [P, N], F32) for d in range(D)]
@@ -180,7 +190,6 @@ def tile_picked_ymsmw_loss_p_kernel(
         nc.vector.scalar_tensor_tensor(step[0][:], tanh[0][:], 1.0, pair[0][:], ALU.add, ALU.mult)
         nc.vector.scalar_tensor_tensor(step[1][:], tanh[1][:], 1.0, scaled[:], ALU.add, ALU.mult)
         nc.scalar.activation(tanh[2][:], half_abs[1][:, 0, :], ACT.Tanh)
-        halves = [slice(b * P, (b + 1) * P) for b in range(BLOCKS)]
         for cols in halves:
             nc.scalar.activation(tanh[3][:, cols], half_abs[1][:, 1, cols], ACT.Tanh)
         for cols in halves:
@@ -191,9 +200,7 @@ def tile_picked_ymsmw_loss_p_kernel(
             nc.vector.scalar_tensor_tensor(step[3][:, cols], tanh[3][:, cols], 1.0, step[2][:, cols], ALU.add, ALU.mult)
         running = step[3]
 
-        capped = tile("capped", [P, N], F32)
-        nc.scalar.activation(capped[:], square[:], ACT.Copy, scale=cap_col[:])
-        cap_sq = ps.tile([P, BLOCKS, V], F32, name="cap_sq")
+        cap_sq = ps.tile([P, BLOCKS, V], F32, name="yd0")
         for b in range(BLOCKS):
             nc.tensor.transpose(cap_sq[:, b, :], capped[:, b * P : (b + 1) * P], ident[:])
 
@@ -201,7 +208,7 @@ def tile_picked_ymsmw_loss_p_kernel(
         for b in range(BLOCKS):
             nc.scalar.activation(growth[:, b, :], log_part[b][:], ACT.Exp)
 
-        turned = [ps.tile([P, V], F32, name=nm) for nm in ("yd0", "yd1")]
+        turned = [ps.tile([P, V], F32, name=nm) for nm in ("yd1", "yd2")]
         weighted = tile("weighted", [P, BLOCKS, V], F32)
         result = tile("result", [P, BLOCKS, V], F32)
         for b in range(BLOCKS):

@@ -46,10 +46,10 @@ def tile_picked_ymsmw_loss_p_kernel(
                 x_scales[0, 4 * q : 4 * q + 4, :].bitcast(I32).partition_broadcast(8),
             )
         treated = tile("treated", [P, D], F32)
-        nc.sync.dma_start(treated[:], trt[0].rearrange("(v d) -> v d", d=D))
+        nc.scalar.dma_start(treated[:], trt[0].rearrange("(v d) -> v d", d=D))
         effect = tile("effect", [P, BLOCKS, 1], F32)
         with nc.allow_non_contiguous_dma(reason="one value a partition and block"):
-            nc.sync.dma_start(effect[:], eff.rearrange("(b p) o -> p b o", p=P))
+            nc.scalar.dma_start(effect[:], eff.rearrange("(b p) o -> p b o", p=P))
         table_words = reuse.tile([P, T], I32, name="table_words", align_bytes=64, offset=0)
         nc.sync.dma_start(table_words[:], x_words[0].rearrange("p c r -> p (c r)").bitcast(I32))
         raw_d = tile("raw_d", [P, PACK, N], F32)
@@ -145,76 +145,84 @@ def tile_picked_ymsmw_loss_p_kernel(
         interleave(nc.vector.tensor_copy, stage_v, raw_n, halves[1])
         quantize(codes_n, scales_n, stage_s, halves[0])
         quantize(codes_n, scales_n, stage_v, halves[1])
-        yn = [ps.tile([P, 2, N], F32, name="yn%d" % h) for h in range(2)]
+        yn = [ps.tile([P, N], F32, name="yn%d" % d) for d in range(D)]
         for d in range(D):
-            product(yn[d // 2][:, d % 2, :], d, codes_n, scales_n)
+            product(yn[d][:], d, codes_n, scales_n)
 
-        log_part = [ps.tile([P, V], F32, name="log_part%d" % b) for b in range(BLOCKS)]
+        def wide(name):
+            return tile(name, [P, N], F32)
+
+        odds = [wide("odds%d" % d) for d in range(D)]
+        inv_chance = [wide("inv_chance%d" % d) for d in range(D)]
+        excess = [wide("excess%d" % d) for d in range(D)]
+        deficit = [wide("deficit%d" % d) for d in range(D)]
+        half_abs = [wide("half_abs%d" % d) for d in range(D)]
+        tanh = [wide("tanh%d" % d) for d in range(D)]
+
+        def make_excess(d):
+            nc.scalar.activation(excess[d][:], yd[d][:], ACT.Relu, scale=neg_sign[:, d : d + 1], bias=neg_clip[:])
+
+        def make_deficit(d):
+            nc.vector.tensor_scalar(deficit[d][:], yn[d][:], sign[:, d : d + 1], 0.0, ALU.mult, ALU.min)
+
+        def times_chance(dst, d, src, cols):
+            nc.vector.scalar_tensor_tensor(dst[:, cols], tanh[d][:, cols], 1.0, src[:, cols], ALU.add, ALU.mult)
 
         def add_turned(src, first, last):
             for b in range(BLOCKS):
-                nc.tensor.matmul(
-                    log_part[b][:], src[:, b * P : (b + 1) * P], ident[:], start=first, stop=last, is_transpose=True
-                )
+                nc.tensor.matmul(log_part[b][:], src[:, halves[b]], ident[:], start=first, stop=last, is_transpose=True)
 
-        odds = [tile("odds%d" % d, [P, N], F32) for d in range(D)]
-        inv_chance = [tile("inv_chance%d" % d, [P, N], F32) for d in range(D)]
-        excess = [tile("excess%d" % d, [P, N], F32) for d in range(D)]
-        deficit = [tile("deficit%d" % d, [P, N], F32) for d in range(D)]
+        whole = slice(0, N)
+        partial = square
         for d in range(D):
             nc.scalar.activation(odds[d][:], yd[d][:], ACT.Exp, scale=neg_sign[:, d : d + 1])
+            if d < 2:
+                make_excess(d)
             nc.vector.tensor_scalar(inv_chance[d][:], odds[d][:], math.exp(CLIP), 1.0, ALU.min, ALU.add)
-        pair = [tile("pair%d" % h, [P, N], F32) for h in range(2)]
-        for h in range(2):
-            nc.vector.tensor_tensor(pair[h][:], inv_chance[2 * h][:], inv_chance[2 * h + 1][:], ALU.mult)
-        for d in range(D):
-            nc.scalar.activation(
-                excess[d][:], yd[d][:], ACT.Relu, scale=neg_sign[:, d : d + 1], bias=neg_clip[:]
-            )
-            add_turned(excess[d], d == 0, False)
-        for d in range(D):
-            nc.vector.tensor_scalar(deficit[d][:], yn[d // 2][:, d % 2, :], sign[:, d : d + 1], 0.0, ALU.mult, ALU.min)
-            add_turned(deficit[d], False, d == D - 1)
+        for d in range(D - 1):
+            grown = wide("grown%d" % d)
+            nc.vector.scalar_tensor_tensor(grown[:], inv_chance[d][:], 0.5, partial[:], ALU.mult, ALU.mult)
+            partial = grown
 
-        half_abs = [tile("half_abs%d" % h, [P, 2, N], F32) for h in range(2)]
-        tanh = [tile("tanh%d" % d, [P, N], F32) for d in range(D)]
-        step = [tile("step%d" % d, [P, N], F32) for d in range(D)]
-        scaled = tile("scaled", [P, N], F32)
-        joined = tile("joined", [P, N], F32)
-        nc.vector.scalar_tensor_tensor(scaled[:], pair[1][:], 0.5**D, square[:], ALU.mult, ALU.mult)
-        for h in range(2):
-            nc.scalar.activation(half_abs[h][:], yn[h][:], ACT.Abs, scale=0.5)
-            if h == 0:
-                for d in range(2):
-                    nc.scalar.activation(tanh[d][:], half_abs[0][:, d, :], ACT.Tanh)
-        nc.vector.scalar_tensor_tensor(step[0][:], tanh[0][:], 1.0, pair[0][:], ALU.add, ALU.mult)
-        nc.vector.scalar_tensor_tensor(step[1][:], tanh[1][:], 1.0, scaled[:], ALU.add, ALU.mult)
-        nc.scalar.activation(tanh[2][:], half_abs[1][:, 0, :], ACT.Tanh)
-        for cols in halves:
-            nc.scalar.activation(tanh[3][:, cols], half_abs[1][:, 1, cols], ACT.Tanh)
-        for cols in halves:
-            nc.vector.tensor_tensor(joined[:, cols], step[0][:, cols], step[1][:, cols], ALU.mult)
-        for cols in halves:
-            nc.vector.scalar_tensor_tensor(step[2][:, cols], tanh[2][:, cols], 1.0, joined[:, cols], ALU.add, ALU.mult)
-        for cols in halves:
-            nc.vector.scalar_tensor_tensor(step[3][:, cols], tanh[3][:, cols], 1.0, step[2][:, cols], ALU.add, ALU.mult)
-        running = step[3]
+        log_part = [ps.tile([P, V], F32, name="yd%d" % b) for b in range(BLOCKS)]
+        add_turned(excess[0], True, False)
+        add_turned(excess[1], False, False)
 
-        cap_sq = ps.tile([P, BLOCKS, V], F32, name="yd0")
+        for d in range(D):
+            nc.scalar.activation(half_abs[d][:], yn[d][:], ACT.Abs, scale=0.5)
+            for cols in halves if d == D - 1 else [whole]:
+                nc.scalar.activation(tanh[d][:, cols], half_abs[d][:, cols], ACT.Tanh)
+        first, second, third, joined, weight = [wide(nm) for nm in ("first", "second", "third", "joined", "weight")]
+        times_chance(first, 0, partial, whole)
+        times_chance(second, 1, inv_chance[D - 1], whole)
+        for cols in halves:
+            times_chance(third, 2, first, cols)
+        for cols in halves:
+            nc.vector.scalar_tensor_tensor(joined[:, cols], third[:, cols], 0.5, second[:, cols], ALU.mult, ALU.mult)
+        for cols in halves:
+            times_chance(weight, 3, joined, cols)
+        for d in range(D):
+            make_deficit(d)
+            add_turned(deficit[d], False, False)
+        for d in (2, 3):
+            make_excess(d)
+            add_turned(excess[d], False, d == D - 1)
+
+        cap_sq = ps.tile([P, BLOCKS, V], F32, name="yn0")
         for b in range(BLOCKS):
-            nc.tensor.transpose(cap_sq[:, b, :], capped[:, b * P : (b + 1) * P], ident[:])
-
+            nc.tensor.transpose(cap_sq[:, b, :], capped[:, halves[b]], ident[:])
         growth = tile("growth", [P, BLOCKS, V], F32)
         for b in range(BLOCKS):
             nc.scalar.activation(growth[:, b, :], log_part[b][:], ACT.Exp)
 
-        turned = [ps.tile([P, V], F32, name=nm) for nm in ("yd1", "yd2")]
+        turned = [ps.tile([P, V], F32, name=nm) for nm in ("yn1", "yn2")]
         weighted = tile("weighted", [P, BLOCKS, V], F32)
-        result = tile("result", [P, BLOCKS, V], F32)
+        result = [tile("result%d" % b, [P, V], F32) for b in range(BLOCKS)]
+        queues = (nc.sync, nc.scalar)
         for b in range(BLOCKS):
-            nc.tensor.transpose(turned[b][:], running[:, b * P : (b + 1) * P], ident[:])
+            nc.tensor.transpose(turned[b][:], weight[:, halves[b]], ident[:])
         for b in range(BLOCKS):
             nc.vector.scalar_tensor_tensor(weighted[:, b, :], growth[:, b, :], BIG, turned[b][:], ALU.min, ALU.mult)
         for b in range(BLOCKS):
-            nc.vector.tensor_tensor(result[:, b, :], weighted[:, b, :], cap_sq[:, b, :], ALU.min)
-        nc.sync.dma_start(out.rearrange("(b p) v -> p b v", p=P), result[:])
+            nc.vector.tensor_tensor(result[b][:], weighted[:, b, :], cap_sq[:, b, :], ALU.min)
+            queues[b].dma_start(out[halves[b], :], result[b][:])

@@ -20,6 +20,7 @@ K, T, S, D, N, V = 512, 2048, 512, 4, 256, 128
 BLOCKS = N // P
 CLIP = 16.0
 BIG = 3.0e38
+HEAD = 768
 
 FLOPS = 2 * 2 * K * N * S
 
@@ -40,30 +41,32 @@ def tile_picked_ymsmw_loss_p_kernel(
         nc.sync.dma_start(offsets[:], offs)
 
         table_scales = tile("table_scales", [P, T], U8)
+        nc.vector.memset(table_scales[:].bitcast(I32), 0)
+        treated = tile("treated", [P, D], F32)
+        nc.sync.dma_start(treated[:], trt[0].rearrange("(v d) -> v d", d=D))
+        table_words = reuse.tile([P, T], I32, name="table_words", align_bytes=64, offset=0)
+        words_in = x_words[0].rearrange("p c r -> p (c r)").bitcast(I32)
+        nc.sync.dma_start(table_words[:, :HEAD], words_in[:, :HEAD])
         for q in range(4):
             nc.sync.dma_start(
-                table_scales[32 * q : 32 * q + 32, :].bitcast(I32),
-                x_scales[0, 4 * q : 4 * q + 4, :].bitcast(I32).partition_broadcast(8),
+                table_scales[32 * q : 32 * q + 4, :].bitcast(I32),
+                x_scales[0, 4 * q : 4 * q + 4, :].bitcast(I32),
             )
-        treated = tile("treated", [P, D], F32)
-        nc.scalar.dma_start(treated[:], trt[0].rearrange("(v d) -> v d", d=D))
-        effect = tile("effect", [P, BLOCKS, 1], F32)
-        with nc.allow_non_contiguous_dma(reason="one value a partition and block"):
-            nc.scalar.dma_start(effect[:], eff.rearrange("(b p) o -> p b o", p=P))
-        table_words = reuse.tile([P, T], I32, name="table_words", align_bytes=64, offset=0)
-        nc.sync.dma_start(table_words[:], x_words[0].rearrange("p c r -> p (c r)").bitcast(I32))
+        nc.sync.dma_start(table_words[:, HEAD:], words_in[:, HEAD:])
         raw_d = tile("raw_d", [P, PACK, N], F32)
         nc.sync.dma_start(raw_d[:], w2.rearrange("(p j) m -> p j m", j=PACK))
         outcome = tile("outcome", [P, BLOCKS, V], F32)
         nc.sync.dma_start(outcome[:], obs.rearrange("(b p) v -> p b v", p=P))
-        cap_col = tile("cap_col", [P, 1], F32)
-        with nc.allow_non_contiguous_dma(reason="one value a partition"):
-            nc.sync.dma_start(cap_col[:], cap[0].rearrange("(v o) -> v o", o=1))
         raw_n = tile("raw_n", [P, PACK, N], F32)
         nc.sync.dma_start(raw_n[:], w1.rearrange("(p j) m -> p j m", j=PACK))
 
+        effect = tile("effect", [P, BLOCKS, 1], F32)
+        cap_col = tile("cap_col", [P, 1], F32)
         ident = tile("ident", [P, P], F32)
-        make_identity(nc, ident[:])
+        with nc.allow_non_contiguous_dma(reason="one value a partition and block"):
+            nc.gpsimd.dma_start(effect[:], eff.rearrange("(b p) o -> p b o", p=P))
+            make_identity(nc, ident[:])
+            nc.gpsimd.dma_start(cap_col[:], cap[0].rearrange("(v o) -> v o", o=1))
 
         sign = tile("sign", [P, D], F32)
         neg_sign = tile("neg_sign", [P, D], F32)
@@ -72,7 +75,7 @@ def tile_picked_ymsmw_loss_p_kernel(
         neg_clip = tile("neg_clip", [P, 1], F32)
         nc.gpsimd.memset(neg_clip[:], -CLIP)
 
-        picked_scales = tile("picked_scales", [P, S], U8)
+        picked_scales = tile("picked", [P, S], U8)
         nc.vector.tensor_copy(picked_scales[:], table_scales[:].indirect(offsets[:]))
         visit_scales = tile("visit_scales", [P, D, V], U8)
         nc.vector.tensor_copy(visit_scales[:], picked_scales[:].rearrange("p (v d) -> p d v", d=D))
@@ -91,7 +94,7 @@ def tile_picked_ymsmw_loss_p_kernel(
             nc.tensor.matmul(resid[:, b, :], outcome[:, b, :], ident[:], start=True, stop=False, is_transpose=True)
             nc.tensor.matmul(resid[:, b, :], shift[:, b, :], ident[:], start=False, stop=True, is_transpose=True)
 
-        visit_words = tile("visit_words", [P, D, V], U32)
+        visit_words = tile("picked", [P, D, V], U32)
         nc.vector.tensor_copy(
             visit_words[:].rearrange("p d v -> p v d"), table_words[:].bitcast(U32).indirect(offsets[:])
         )

import math
from contextlib import ExitStack

import concourse.mybir as mybir
from concourse.masks import make_identity

F32 = mybir.dt.float32
BF16 = mybir.dt.bfloat16
I32 = mybir.dt.int32
U32 = mybir.dt.uint32
U16 = mybir.dt.uint16
U8 = mybir.dt.uint8
FP8X4 = mybir.dt.float8_e4m3fn_x4
ALU = mybir.AluOpType
ACT = mybir.ActivationFunctionType

P = 128
PACK = 4
K, T, S, D, N, V = 512, 2048, 512, 4, 256, 128
BLOCKS = N // P
CLIP = 16.0
BIG = 3.0e38
HEAD = 768

FLOPS = 2 * 2 * K * N * S


def tile_picked_ymsmw_loss_p_kernel(
    tc, x_words, x_scales, w1, w2, trt, cap, obs, eff, offs, out
):
    nc = tc.nc
    with ExitStack() as ctx:
        sb = ctx.enter_context(tc.tile_pool(name="sb", bufs=1))
        reuse = ctx.enter_context(tc.tile_pool(name="reuse", bufs=1))
        ps = ctx.enter_context(tc.psum_pool(name="ps", bufs=1))

        def tile(name, shape, dtype):
            return sb.tile(shape, dtype, name=name, align_bytes=64)

        offsets = tile("offsets", [P, S // 16], U16)
        nc.sync.dma_start(offsets[:], offs)

        table_scales = tile("table_scales", [P, T], U8)
        nc.vector.memset(table_scales[:].bitcast(I32), 0)
        treated = tile("treated", [P, D], F32)
        nc.sync.dma_start(treated[:], trt[0].rearrange("(v d) -> v d", d=D))
        table_words = reuse.tile([P, T], I32, name="table_words", align_bytes=64, offset=0)
        words_in = x_words[0].rearrange("p c r -> p (c r)").bitcast(I32)
        nc.sync.dma_start(table_words[:, :HEAD], words_in[:, :HEAD])
        for q in range(4):
            nc.sync.dma_start(
                table_scales[32 * q : 32 * q + 4, :].bitcast(I32),
                x_scales[0, 4 * q : 4 * q + 4, :].bitcast(I32),
            )
        nc.sync.dma_start(table_words[:, HEAD:], words_in[:, HEAD:])
        raw_d = tile("raw_d", [P, PACK, N], F32)
        nc.sync.dma_start(raw_d[:], w2.rearrange("(p j) m -> p j m", j=PACK))
        outcome = tile("outcome", [P, BLOCKS, V], F32)
        nc.sync.dma_start(outcome[:], obs.rearrange("(b p) v -> p b v", p=P))
        raw_n = tile("raw_n", [P, PACK, N], F32)
        nc.sync.dma_start(raw_n[:], w1.rearrange("(p j) m -> p j m", j=PACK))

        effect = tile("effect", [P, BLOCKS, 1], F32)
        cap_col = tile("cap_col", [P, 1], F32)
        ident = tile("ident", [P, P], F32)
        with nc.allow_non_contiguous_dma(reason="one value a partition and block"):
            nc.gpsimd.dma_start(effect[:], eff.rearrange("(b p) o -> p b o", p=P))
            make_identity(nc, ident[:])
            nc.gpsimd.dma_start(cap_col[:], cap[0].rearrange("(v o) -> v o", o=1))

        sign = tile("sign", [P, D], F32)
        neg_sign = tile("neg_sign", [P, D], F32)
        nc.scalar.activation(neg_sign[:], treated[:], ACT.Copy, bias=1.0, scale=-2.0)
        nc.scalar.activation(sign[:], treated[:], ACT.Copy, bias=-1.0, scale=2.0)
        neg_clip = tile("neg_clip", [P, 1], F32)
        nc.gpsimd.memset(neg_clip[:], -CLIP)

        picked_scales = tile("picked", [P, S], U8)
        nc.vector.tensor_copy(picked_scales[:], table_scales[:].indirect(offsets[:]))
        visit_scales = tile("visit_scales", [P, D, V], U8)
        nc.vector.tensor_copy(visit_scales[:], picked_scales[:].rearrange("p (v d) -> p d v", d=D))

        share = tile("share", [P, D], F32)
        neg_mean = tile("neg_mean", [P, 1], F32)
        nc.scalar.activation(share[:], treated[:], ACT.Copy, scale=-1.0 / D, accum_out=neg_mean[:])
        spread = ps.tile([P, V], F32, name="yn0")
        nc.tensor.transpose(spread[:], neg_mean[:].to_broadcast([P, P]), ident[:])
        shift = tile("shift", [P, BLOCKS, V], F32)
        for b in range(BLOCKS):
            nc.scalar.activation(shift[:, b, :], spread[:], ACT.Copy, scale=effect[:, b, :])

        resid = ps.tile([P, BLOCKS, P], F32, name="yn1")
        for b in range(BLOCKS):
            nc.tensor.matmul(resid[:, b, :], outcome[:, b, :], ident[:], start=True, stop=False, is_transpose=True)
            nc.tensor.matmul(resid[:, b, :], shift[:, b, :], ident[:], start=False, stop=True, is_transpose=True)

        visit_words = tile("picked", [P, D, V], U32)
        nc.vector.tensor_copy(
            visit_words[:].rearrange("p d v -> p v d"), table_words[:].bitcast(U32).indirect(offsets[:])
        )

        halves = [slice(b * P, (b + 1) * P) for b in range(BLOCKS)]

        def interleave(copy, grouped, raw, cols):
            copy(
                grouped[:].rearrange("p (c i) j -> p c j i", i=4),
                raw[:, :, cols].rearrange("p j (c i) -> p c j i", i=4),
            )

        def quantize(codes, scales, grouped, cols):
            nc.vector.quantize_mx(
                out=codes[:, cols].bitcast(FP8X4), scales=scales[:, cols], in_=grouped[:].rearrange("p m j -> p (m j)")
            )

        def product(bank, d, codes, scales):
            nc.tensor.matmul_mx(
                out=bank,
                lhsT=visit_words[:, d, :].bitcast(FP8X4),
                lhsT_scale=visit_scales[:, d, :],
                rhs=codes[:].bitcast(FP8X4),
                rhs_scale=scales[:],
                start=True,
                stop=True,
            )

        stage_s = reuse.tile([P, P, PACK], BF16, name="stage_sd", align_bytes=64, offset=8192)
        stage_v = reuse.tile([P, P, PACK], BF16, name="stage_vd", align_bytes=64, offset=7168)
        codes_d = reuse.tile([P, N], U32, name="codes_d", align_bytes=64, offset=2048)
        scales_d = tile("scales_d", [P, N], U8)
        interleave(nc.scalar.copy, stage_s, raw_d, halves[0])
        interleave(nc.vector.tensor_copy, stage_v, raw_d, halves[1])
        quantize(codes_d, scales_d, stage_s, halves[0])
        quantize(codes_d, scales_d, stage_v, halves[1])
        yd = [ps.tile([P, N], F32, name="yd%d" % d) for d in range(D)]
        for d in range(D):
            product(yd[d][:], d, codes_d, scales_d)

        square = tile("raw_d", [P, N], F32)
        nc.scalar.activation(square[:], resid[:].rearrange("p b m -> p (b m)"), ACT.Square)
        capped = tile("capped", [P, N], F32)
        nc.scalar.activation(capped[:], square[:], ACT.Copy, scale=cap_col[:])

        stage_s = tile("stage_n", [P, P, PACK], BF16)
        stage_v = reuse.tile([P, P, PACK], BF16, name="stage_vn", align_bytes=64, offset=7680)
        codes_n = reuse.tile([P, N], U32, name="codes_n", align_bytes=64, offset=8704)
        scales_n = reuse.tile([P, N], U8, name="scales_n", align_bytes=64, offset=7168)
        interleave(nc.scalar.copy, stage_s, raw_n, halves[0])
        interleave(nc.vector.tensor_copy, stage_v, raw_n, halves[1])
        quantize(codes_n, scales_n, stage_s, halves[0])
        quantize(codes_n, scales_n, stage_v, halves[1])
        yn = [ps.tile([P, N], F32, name="yn%d" % d) for d in range(D)]
        for d in range(D):
            product(yn[d][:], d, codes_n, scales_n)

        def wide(name):
            return tile(name, [P, N], F32)

        odds = [wide("odds%d" % d) for d in range(D)]
        inv_chance = [wide("inv_chance%d" % d) for d in range(D)]
        excess = [wide("excess%d" % d) for d in range(D)]
        deficit = [wide("deficit%d" % d) for d in range(D)]
        half_abs = [wide("half_abs%d" % d) for d in range(D)]
        tanh = [wide("tanh%d" % d) for d in range(D)]

        def make_excess(d):
            nc.scalar.activation(excess[d][:], yd[d][:], ACT.Relu, scale=neg_sign[:, d : d + 1], bias=neg_clip[:])

        def make_deficit(d):
            nc.vector.tensor_scalar(deficit[d][:], yn[d][:], sign[:, d : d + 1], 0.0, ALU.mult, ALU.min)

        def times_chance(dst, d, src, cols):
            nc.vector.scalar_tensor_tensor(dst[:, cols], tanh[d][:, cols], 1.0, src[:, cols], ALU.add, ALU.mult)

        def add_turned(src, first, last):
            for b in range(BLOCKS):
                nc.tensor.matmul(log_part[b][:], src[:, halves[b]], ident[:], start=first, stop=last, is_transpose=True)

        whole = slice(0, N)
        partial = square
        for d in range(D):
            nc.scalar.activation(odds[d][:], yd[d][:], ACT.Exp, scale=neg_sign[:, d : d + 1])
            if d < 2:
                make_excess(d)
            nc.vector.tensor_scalar(inv_chance[d][:], odds[d][:], math.exp(CLIP), 1.0, ALU.min, ALU.add)
        for d in range(D - 1):
            grown = wide("grown%d" % d)
            nc.vector.scalar_tensor_tensor(grown[:], inv_chance[d][:], 0.5, partial[:], ALU.mult, ALU.mult)
            partial = grown

        log_part = [ps.tile([P, V], F32, name="yd%d" % b) for b in range(BLOCKS)]
        add_turned(excess[0], True, False)
        add_turned(excess[1], False, False)

        for d in range(D):
            nc.scalar.activation(half_abs[d][:], yn[d][:], ACT.Abs, scale=0.5)
            for cols in halves if d == D - 1 else [whole]:
                nc.scalar.activation(tanh[d][:, cols], half_abs[d][:, cols], ACT.Tanh)
        first, second, third, joined, weight = [wide(nm) for nm in ("first", "second", "third", "joined", "weight")]
        times_chance(first, 0, partial, whole)
        times_chance(second, 1, inv_chance[D - 1], whole)
        for cols in halves:
            times_chance(third, 2, first, cols)
        for cols in halves:
            nc.vector.scalar_tensor_tensor(joined[:, cols], third[:, cols], 0.5, second[:, cols], ALU.mult, ALU.mult)
        for cols in halves:
            times_chance(weight, 3, joined, cols)
        for d in range(D):
            make_deficit(d)
            add_turned(deficit[d], False, False)
        for d in (2, 3):
            make_excess(d)
            add_turned(excess[d], False, d == D - 1)

        cap_sq = ps.tile([P, BLOCKS, V], F32, name="yn0")
        for b in range(BLOCKS):
            nc.tensor.transpose(cap_sq[:, b, :], capped[:, halves[b]], ident[:])
        growth = tile("growth", [P, BLOCKS, V], F32)
        for b in range(BLOCKS):
            nc.scalar.activation(growth[:, b, :], log_part[b][:], ACT.Exp)

        turned = [ps.tile([P, V], F32, name=nm) for nm in ("yn1", "yn2")]
        weighted = tile("weighted", [P, BLOCKS, V], F32)
        result = [tile("result%d" % b, [P, V], F32) for b in range(BLOCKS)]
        queues = (nc.sync, nc.scalar)
        for b in range(BLOCKS):
            nc.tensor.transpose(turned[b][:], weight[:, halves[b]], ident[:])
        for b in range(BLOCKS):
            nc.vector.scalar_tensor_tensor(weighted[:, b, :], growth[:, b, :], BIG, turned[b][:], ALU.min, ALU.mult)
        for b in range(BLOCKS):
            nc.vector.tensor_tensor(result[b][:], weighted[:, b, :], cap_sq[:, b, :], ALU.min)
            queues[b].dma_start(out[halves[b], :], result[b][:])
